import numpy as np
import ml_dtypes


def mxq(x, axis, fmt="e4m3"):
    dtype, down = {"e4m3": (ml_dtypes.float8_e4m3fn, 7), "e5m2": (ml_dtypes.float8_e5m2, 14)}[fmt]
    v = np.moveaxis(np.asarray(x, np.float32).astype(ml_dtypes.bfloat16).astype(np.float64), axis, -1)
    blocks = v.reshape(v.shape[:-1] + (-1, 32))
    amax = np.abs(blocks).max(-1, keepdims=True)
    byte = np.maximum(np.where(amax > 0, np.frexp(amax)[1] - 1 + 127, 0) - down, 1)
    scale = np.exp2(byte - 127.0)
    codes = (blocks / scale).astype(np.float32).astype(dtype).astype(np.float64)
    return np.moveaxis((codes * scale).reshape(v.shape), -1, axis)


WIDE = False


def mx_kscale(k):
    if not WIDE:
        return np.ones(k)
    levels = np.array([10, -10, 5, -5, 0])
    if k % 512:
        return np.exp2(np.random.permutation(np.resize(levels, k // 32))).repeat(32)
    a = np.empty((k // 512, 16))
    for p in range(k // 512):
        a[p, :8] = np.random.permutation(np.resize(levels, 8))
        for g in range(8):
            far = levels[np.abs(levels - a[p, g]) >= 10]
            a[p, g + 8] = far[np.random.randint(len(far))]
    return np.exp2(a.ravel()).repeat(32)


def f64(x):
    return np.asarray(x).astype(np.float64)


def striped(idx):
    return np.tile(idx.reshape(-1, 16).T, (8, 1)).astype(np.uint16)


def unstriped(offs):
    return offs[:16].T.reshape(-1).astype(np.int64)


E2M1 = np.array([0.0, 0.5, 1.0, 1.5, 2.0, 3.0, 4.0, 6.0, -0.0, -0.5, -1.0, -1.5, -2.0, -3.0, -4.0, -6.0])


def pack_weight(w, fmt):
    k, n = w.shape
    w = f64(np.asarray(w, np.float32).astype(ml_dtypes.bfloat16)).reshape(k // 32, 32, n)
    amax = np.abs(w).max(1)
    if fmt == "e4m3":
        byte = np.frexp(amax)[1] - 1 + 127 - 7
    else:
        mant, ex = np.frexp(amax / 6.0)
        byte = np.where(mant > 0.5, ex, ex - 1) + 127
    byte = np.clip(np.where(amax > 0, byte, 1), 1, 254)
    scaled = (w * np.exp2(127.0 - byte)[:, None, :]).reshape(k, n).astype(np.float32)
    by_word = np.ascontiguousarray(scaled.reshape(k // 512, 128, 4, n).transpose(0, 1, 3, 2))
    if fmt == "e4m3":
        words = by_word.astype(ml_dtypes.float8_e4m3fn).view(np.uint8)
    else:
        c = by_word.astype(ml_dtypes.float4_e2m1fn).view(np.uint8) & 0xF
        words = (c[..., 0::2] | (c[..., 1::2] << 4)).reshape(k // 512, 128, 2 * n)
    return np.ascontiguousarray(words), np.ascontiguousarray(byte.astype(np.uint8).reshape(k // 512, 16, n))


def unpack_weight(words, scales, fmt):
    g, _, n = scales.shape
    words = np.ascontiguousarray(words).reshape(g, 128, n, -1)
    if fmt == "e4m3":
        vals = words.view(ml_dtypes.float8_e4m3fn).astype(np.float64)
    else:
        nib = np.empty((g, 128, n, 4), np.uint8)
        nib[..., 0::2] = words & 0xF
        nib[..., 1::2] = words >> 4
        vals = E2M1[nib]
    vals = vals * np.repeat(np.exp2(scales.astype(np.float64) - 127.0), 8, axis=1)[..., None]
    return vals.transpose(0, 1, 3, 2).reshape(g * 512, n)


def relu(v):
    return np.maximum(v, 0.0)


K, T, S, H, N = 512, 1024, 512, 512, 256


def setup_inputs():
    n = np.random.standard_normal
    s = mx_kscale(K)
    u = mx_kscale(H)
    hard = np.random.permutation(T)[:S]
    x = pack_weight(n((K, T)) * s[:, None], "e4m3")
    w = pack_weight(n((K, N)) / np.sqrt(K) / s[:, None], "e2m1")
    w1 = pack_weight(n((K, H)) / np.sqrt(K) / s[:, None] * u, "e2m1")
    w2 = pack_weight(n((H, N)) / np.sqrt(H) / u[:, None], "e2m1")
    return {
        "x_words": x[0],
        "x_scales": x[1],
        "w_words": w[0],
        "w_scales": w[1],
        "w1_words": w1[0],
        "w1_scales": w1[1],
        "w2_words": w2[0],
        "w2_scales": w2[1],
        "offs": striped(hard),
    }


def reference(x_words, x_scales, w_words, w_scales, w1_words, w1_scales, w2_words, w2_scales, offs):
    w = unpack_weight(w_words, w_scales, "e2m1")
    w1 = unpack_weight(w1_words, w1_scales, "e2m1")
    w2 = unpack_weight(w2_words, w2_scales, "e2m1")
    idx = unstriped(offs)
    x = unpack_weight(x_words, x_scales, "e4m3")
    out = w.T @ x
    h = relu(w1.T @ x[:, idx])
    out[:, idx] = w2.T @ mxq(h, 0, "e4m3")
    return out

@@ -1,0 +1,169 @@
+from contextlib import ExitStack
+
+import concourse.mybir as mybir
+
+K, T, S, H, N = 512, 1024, 512, 512, 256
+FLOPS = 2 * K * N * T + 2 * K * H * S + 2 * H * N * S
+
+F32 = mybir.dt.float32
+BF16 = mybir.dt.bfloat16
+I32 = mybir.dt.int32
+U32 = mybir.dt.uint32
+U16 = mybir.dt.uint16
+U8 = mybir.dt.uint8
+FP8X4 = mybir.dt.float8_e4m3fn_x4
+FP4X4 = mybir.dt.float4_e2m1fn_x4
+RELU = mybir.ActivationFunctionType.Relu
+COPY = mybir.ActivationFunctionType.Copy
+
+P = 128
+PACK = 4
+CHUNK = 128
+CHUNKS = S // CHUNK
+BANK = 512
+
+
+def load_scale_rows(queue, plane, scales):
+    for q in range(4):
+        queue.dma_start(out=plane[32 * q : 32 * q + 4, :].bitcast(I32), in_=scales[0, 4 * q : 4 * q + 4, :].bitcast(I32))
+
+
+def tile_moe_cas_mlp_relu_kernel(
+    tc, x_words, x_scales, w_words, w_scales, w1_words, w1_scales, w2_words, w2_scales, offs, out
+):
+    nc = tc.nc
+    with ExitStack() as ctx:
+        keep = ctx.enter_context(tc.tile_pool(name="keep", bufs=1))
+        psum_y = ctx.enter_context(tc.psum_pool(name="psum_y", bufs=2))
+        psum_h = ctx.enter_context(tc.psum_pool(name="psum_h", bufs=3))
+        psum_z = ctx.enter_context(tc.psum_pool(name="psum_z", bufs=3))
+
+        offsets = keep.tile([P, S // 16], U16, name="offsets")
+        xw = keep.tile([P, T], I32, name="xw", align_bytes=64)
+        xs = keep.tile([P, T], U8, name="xs", align_bytes=64)
+        ww = keep.tile([P, 2 * N], U8, name="ww", align_bytes=64)
+        w1w_raw = keep.tile([P, 2 * H], U8, name="w1w_raw", align_bytes=64)
+        w1w = keep.tile([P, 2 * H], U8, name="w1w", align_bytes=64)
+        w2w = keep.tile([P, 2 * N], U8, name="w2w", align_bytes=64)
+        w1s_raw = keep.tile([P, H], U8, name="w1s_raw", align_bytes=64)
+        w1s = keep.tile([P, H], U8, name="w1s", align_bytes=64)
+        wns = keep.tile([P, 2 * N], U8, name="wns", align_bytes=64)
+        gw = keep.tile([P, S], U32, name="gw", align_bytes=64)
+        gs = keep.tile([P, S], U8, name="gs", align_bytes=64)
+        hb = keep.tile([P, S, PACK], BF16, name="hb", align_bytes=64)
+        hw = keep.tile([P, S], U32, name="hw", align_bytes=64)
+        hs = keep.tile([P, S], U8, name="hs", align_bytes=64)
+        z = keep.tile([P, 2, S], F32, name="z", align_bytes=64)
+        res = [keep.tile([P, T], F32, name="res%d" % m, align_bytes=64) for m in range(2)]
+        warm = keep.tile([P, 8], F32, name="warm")
+
+        ws = wns[:, 0:N]
+        w2s = wns[:, N : 2 * N]
+
+        nc.vector.memset(w1s_raw[:].bitcast(I32), 0)
+        nc.vector.memset(xs[:].bitcast(I32), 0)
+        nc.vector.memset(wns[:].bitcast(I32), 0)
+        nc.vector.memset(warm[:], 0.0)
+
+        nc.sync.dma_start(out=w1w_raw[:].bitcast(I32), in_=w1_words[0].bitcast(I32))
+        load_scale_rows(nc.scalar, w1s_raw[:], w1_scales)
+        nc.sync.dma_start(out=xw[:], in_=x_words[0].rearrange("p t d -> p (t d)").bitcast(I32))
+        nc.sync.dma_start(offsets[:], offs)
+        load_scale_rows(nc.sync, xs[:], x_scales)
+        nc.gpsimd.dma_start(out=ww[:].bitcast(I32), in_=w_words[0].bitcast(I32))
+        nc.gpsimd.dma_start(out=w2w[:].bitcast(I32), in_=w2_words[0].bitcast(I32))
+        load_scale_rows(nc.sync, ws, w_scales)
+        load_scale_rows(nc.sync, w2s, w2_scales)
+
+        nc.scalar.activation(out=warm[:], in_=warm[:], func=RELU)
+
+        nc.vector.tensor_copy(
+            out=w1w[:].bitcast(U16).rearrange("p (t m) -> p t m", t=PACK),
+            in_=w1w_raw[:].bitcast(U16).rearrange("p (m t) -> p t m", t=PACK),
+        )
+        nc.vector.tensor_copy(
+            out=w1s[:].rearrange("p (t m) -> p t m", t=PACK),
+            in_=w1s_raw[:].rearrange("p (m t) -> p t m", t=PACK),
+        )
+
+        def slots(c):
+            return slice(c * CHUNK, (c + 1) * CHUNK)
+
+        def listed(a, b):
+            return offsets[:, a // 16 : b // 16]
+
+        def light(m, half):
+            cols = slice(half * BANK, (half + 1) * BANK)
+            acc = psum_y.tile([P, BANK], F32, name="acc_y")
+            nc.tensor.matmul_mx(
+                out=acc[:],
+                lhsT=ww[:, 2 * P * m : 2 * P * (m + 1)].bitcast(FP4X4),
+                lhsT_scale=ws[:, P * m : P * (m + 1)],
+                rhs=xw[:, cols].bitcast(FP8X4),
+                rhs_scale=xs[:, cols],
+                start=True,
+                stop=True,
+            )
+            nc.scalar.activation(out=res[m][:, cols], in_=acc[:], func=COPY)
+
+        def first(c):
+            cols = slots(c)
+            lst = listed(c * CHUNK, (c + 1) * CHUNK)
+            nc.vector.tensor_copy(out=gw[:, cols], in_=xw[:].bitcast(U32).indirect(lst))
+            nc.vector.tensor_copy(out=gs[:, cols], in_=xs[:].indirect(lst))
+            acc = psum_h.tile([P, PACK, CHUNK], F32, name="acc_h")
+            for t in range(PACK):
+                nc.tensor.matmul_mx(
+                    out=acc[:, t, :],
+                    lhsT=w1w[:, 2 * P * t : 2 * P * (t + 1)].bitcast(FP4X4),
+                    lhsT_scale=w1s[:, P * t : P * (t + 1)],
+                    rhs=gw[:, cols].bitcast(FP8X4),
+                    rhs_scale=gs[:, cols],
+                    start=True,
+                    stop=True,
+                )
+            nc.scalar.activation(out=hb[:, cols, :], in_=acc[:].rearrange("p t j -> p j t"), func=RELU)
+
+        def quantise(c):
+            cols = slots(c)
+            nc.vector.quantize_mx(
+                out=hw[:, cols].bitcast(FP8X4),
+                scales=hs[:, cols],
+                in_=hb[:, cols, :].rearrange("p j t -> p (j t)"),
+            )
+
+        def second(m, a, b):
+            acc = psum_z.tile([P, BANK], F32, name="acc_z")
+            nc.tensor.matmul_mx(
+                out=acc[:, 0 : b - a],
+                lhsT=w2w[:, 2 * P * m : 2 * P * (m + 1)].bitcast(FP4X4),
+                lhsT_scale=w2s[:, P * m : P * (m + 1)],
+                rhs=hw[:, a:b].bitcast(FP8X4),
+                rhs_scale=hs[:, a:b],
+                start=True,
+                stop=True,
+            )
+            nc.scalar.activation(out=z[:, m, a:b], in_=acc[:, 0 : b - a], func=COPY)
+
+        def scatter(m, a, b):
+            nc.vector.tensor_copy(out=res[m][:].indirect(listed(a, b)), in_=z[:, m, a:b])
+
+        first(0)
+        light(0, 0)
+        first(1)
+        quantise(0)
+        second(0, 0, CHUNK)
+        light(0, 1)
+        for c in range(1, CHUNKS):
+            if c + 1 < CHUNKS:
+                first(c + 1)
+            quantise(c)
+            second(0, c * CHUNK, (c + 1) * CHUNK)
+        second(1, 0, S)
+        light(1, 0)
+        light(1, 1)
+        for c in range(CHUNKS):
+            scatter(0, c * CHUNK, (c + 1) * CHUNK)
+        nc.sync.dma_start(out=out[0:P, :], in_=res[0][:])
+        scatter(1, 0, S)
+        nc.sync.dma_start(out=out[P : 2 * P, :], in_=res[1][:])

@@ -23,9 +23,8 @@ CHUNKS = S // CHUNK
 BANK = 512
 
 
-def load_scale_rows(queue, plane, scales):
-    for q in range(4):
-        queue.dma_start(out=plane[32 * q : 32 * q + 4, :].bitcast(I32), in_=scales[0, 4 * q : 4 * q + 4, :].bitcast(I32))
+def load_scale_rows(queue, plane, scales, q):
+    queue.dma_start(out=plane[32 * q : 32 * q + 4, :].bitcast(I32), in_=scales[0, 4 * q : 4 * q + 4, :].bitcast(I32))
 
 
 def tile_moe_cas_mlp_relu_kernel(
@@ -34,6 +33,7 @@ def tile_moe_cas_mlp_relu_kernel(
     nc = tc.nc
     with ExitStack() as ctx:
         keep = ctx.enter_context(tc.tile_pool(name="keep", bufs=1))
+        ring = ctx.enter_context(tc.tile_pool(name="ring", bufs=2))
         psum_y = ctx.enter_context(tc.psum_pool(name="psum_y", bufs=2))
         psum_h = ctx.enter_context(tc.psum_pool(name="psum_h", bufs=3))
         psum_z = ctx.enter_context(tc.psum_pool(name="psum_z", bufs=3))
@@ -45,37 +45,41 @@ def tile_moe_cas_mlp_relu_kernel(
         w1w_raw = keep.tile([P, 2 * H], U8, name="w1w_raw", align_bytes=64)
         w1w = keep.tile([P, 2 * H], U8, name="w1w", align_bytes=64)
         w2w = keep.tile([P, 2 * N], U8, name="w2w", align_bytes=64)
-        w1s_raw = keep.tile([P, H], U8, name="w1s_raw", align_bytes=64)
         w1s = keep.tile([P, H], U8, name="w1s", align_bytes=64)
-        wns = keep.tile([P, 2 * N], U8, name="wns", align_bytes=64)
-        gw = keep.tile([P, S], U32, name="gw", align_bytes=64)
+        wns = keep.tile([P, H + 2 * N], U8, name="wns", align_bytes=64)
         gs = keep.tile([P, S], U8, name="gs", align_bytes=64)
         hb = keep.tile([P, S, PACK], BF16, name="hb", align_bytes=64)
         hw = keep.tile([P, S], U32, name="hw", align_bytes=64)
         hs = keep.tile([P, S], U8, name="hs", align_bytes=64)
         z = keep.tile([P, 2, S], F32, name="z", align_bytes=64)
         res = [keep.tile([P, T], F32, name="res%d" % m, align_bytes=64) for m in range(2)]
-        warm = keep.tile([P, 8], F32, name="warm")
 
-        ws = wns[:, 0:N]
-        w2s = wns[:, N : 2 * N]
+        w1s_raw = wns[:, 0:H]
+        ws = wns[:, H : H + N]
+        w2s = wns[:, H + N : H + 2 * N]
 
-        nc.vector.memset(w1s_raw[:].bitcast(I32), 0)
         nc.vector.memset(xs[:].bitcast(I32), 0)
         nc.vector.memset(wns[:].bitcast(I32), 0)
-        nc.vector.memset(warm[:], 0.0)
 
-        nc.sync.dma_start(out=w1w_raw[:].bitcast(I32), in_=w1_words[0].bitcast(I32))
-        load_scale_rows(nc.scalar, w1s_raw[:], w1_scales)
-        nc.sync.dma_start(out=xw[:], in_=x_words[0].rearrange("p t d -> p (t d)").bitcast(I32))
         nc.sync.dma_start(offsets[:], offs)
-        load_scale_rows(nc.sync, xs[:], x_scales)
+        nc.sync.dma_start(out=w1w_raw[:].bitcast(I32), in_=w1_words[0].bitcast(I32))
+        load_scale_rows(nc.sync, xs[:], x_scales, 0)
+        nc.sync.dma_start(out=xw[:], in_=x_words[0].rearrange("p t d -> p (t d)").bitcast(I32))
+        for q in range(4):
+            load_scale_rows(nc.scalar, w1s_raw, w1_scales, q)
+        load_scale_rows(nc.scalar, xs[:], x_scales, 1)
+        load_scale_rows(nc.sync, xs[:], x_scales, 2)
+        load_scale_rows(nc.scalar, xs[:], x_scales, 3)
+        load_scale_rows(nc.sync, ws, w_scales, 0)
+        load_scale_rows(nc.scalar, ws, w_scales, 1)
+        load_scale_rows(nc.sync, ws, w_scales, 2)
         nc.gpsimd.dma_start(out=ww[:].bitcast(I32), in_=w_words[0].bitcast(I32))
+        load_scale_rows(nc.gpsimd, ws, w_scales, 3)
         nc.gpsimd.dma_start(out=w2w[:].bitcast(I32), in_=w2_words[0].bitcast(I32))
-        load_scale_rows(nc.sync, ws, w_scales)
-        load_scale_rows(nc.sync, w2s, w2_scales)
-
-        nc.scalar.activation(out=warm[:], in_=warm[:], func=RELU)
+        load_scale_rows(nc.gpsimd, w2s, w2_scales, 0)
+        load_scale_rows(nc.sync, w2s, w2_scales, 1)
+        load_scale_rows(nc.sync, w2s, w2_scales, 2)
+        load_scale_rows(nc.sync, w2s, w2_scales, 3)
 
         nc.vector.tensor_copy(
             out=w1w[:].bitcast(U16).rearrange("p (t m) -> p t m", t=PACK),
@@ -83,7 +87,7 @@ def tile_moe_cas_mlp_relu_kernel(
         )
         nc.vector.tensor_copy(
             out=w1s[:].rearrange("p (t m) -> p t m", t=PACK),
-            in_=w1s_raw[:].rearrange("p (m t) -> p t m", t=PACK),
+            in_=w1s_raw.rearrange("p (m t) -> p t m", t=PACK),
         )
 
         def slots(c):
@@ -109,7 +113,8 @@ def tile_moe_cas_mlp_relu_kernel(
         def first(c):
             cols = slots(c)
             lst = listed(c * CHUNK, (c + 1) * CHUNK)
-            nc.vector.tensor_copy(out=gw[:, cols], in_=xw[:].bitcast(U32).indirect(lst))
+            gw = ring.tile([P, CHUNK], U32, name="gw", align_bytes=64)
+            nc.vector.tensor_copy(out=gw[:], in_=xw[:].bitcast(U32).indirect(lst))
             nc.vector.tensor_copy(out=gs[:, cols], in_=xs[:].indirect(lst))
             acc = psum_h.tile([P, PACK, CHUNK], F32, name="acc_h")
             for t in range(PACK):
@@ -117,7 +122,7 @@ def tile_moe_cas_mlp_relu_kernel(
                     out=acc[:, t, :],
                     lhsT=w1w[:, 2 * P * t : 2 * P * (t + 1)].bitcast(FP4X4),
                     lhsT_scale=w1s[:, P * t : P * (t + 1)],
-                    rhs=gw[:, cols].bitcast(FP8X4),
+                    rhs=gw[:].bitcast(FP8X4),
                     rhs_scale=gs[:, cols],
                     start=True,
                     stop=True,

@@ -34,9 +34,7 @@ def tile_moe_cas_mlp_relu_kernel(
     with ExitStack() as ctx:
         keep = ctx.enter_context(tc.tile_pool(name="keep", bufs=1))
         ring = ctx.enter_context(tc.tile_pool(name="ring", bufs=2))
-        psum_y = ctx.enter_context(tc.psum_pool(name="psum_y", bufs=2))
-        psum_h = ctx.enter_context(tc.psum_pool(name="psum_h", bufs=3))
-        psum_z = ctx.enter_context(tc.psum_pool(name="psum_z", bufs=3))
+        psum = ctx.enter_context(tc.psum_pool(name="psum", bufs=1))
 
         offsets = keep.tile([P, S // 16], U16, name="offsets")
         xw = keep.tile([P, T], I32, name="xw", align_bytes=64)
@@ -46,7 +44,9 @@ def tile_moe_cas_mlp_relu_kernel(
         w1w = keep.tile([P, 2 * H], U8, name="w1w", align_bytes=64)
         w2w = keep.tile([P, 2 * N], U8, name="w2w", align_bytes=64)
         w1s = keep.tile([P, H], U8, name="w1s", align_bytes=64)
-        wns = keep.tile([P, H + 2 * N], U8, name="wns", align_bytes=64)
+        w1s_raw = keep.tile([P, H], U8, name="w1s_raw", align_bytes=64)
+        wns = keep.tile([P, 2 * N], U8, name="wns", align_bytes=64)
+        warm = keep.tile([P, 8], F32, name="warm")
         gs = keep.tile([P, S], U8, name="gs", align_bytes=64)
         hb = keep.tile([P, S, PACK], BF16, name="hb", align_bytes=64)
         hw = keep.tile([P, S], U32, name="hw", align_bytes=64)
@@ -54,32 +54,29 @@ def tile_moe_cas_mlp_relu_kernel(
         z = keep.tile([P, 2, S], F32, name="z", align_bytes=64)
         res = [keep.tile([P, T], F32, name="res%d" % m, align_bytes=64) for m in range(2)]
 
-        w1s_raw = wns[:, 0:H]
-        ws = wns[:, H : H + N]
-        w2s = wns[:, H + N : H + 2 * N]
+        ws = wns[:, 0:N]
+        w2s = wns[:, N : 2 * N]
 
+        nc.vector.memset(w1s_raw[:].bitcast(I32), 0)
         nc.vector.memset(xs[:].bitcast(I32), 0)
+        nc.vector.memset(warm[:], 0.0)
         nc.vector.memset(wns[:].bitcast(I32), 0)
 
         nc.sync.dma_start(offsets[:], offs)
-        nc.sync.dma_start(out=w1w_raw[:].bitcast(I32), in_=w1_words[0].bitcast(I32))
-        load_scale_rows(nc.sync, xs[:], x_scales, 0)
-        nc.sync.dma_start(out=xw[:], in_=x_words[0].rearrange("p t d -> p (t d)").bitcast(I32))
+        nc.scalar.dma_start(out=w1w_raw[:].bitcast(I32), in_=w1_words[0].bitcast(I32))
         for q in range(4):
-            load_scale_rows(nc.scalar, w1s_raw, w1_scales, q)
-        load_scale_rows(nc.scalar, xs[:], x_scales, 1)
-        load_scale_rows(nc.sync, xs[:], x_scales, 2)
-        load_scale_rows(nc.scalar, xs[:], x_scales, 3)
-        load_scale_rows(nc.sync, ws, w_scales, 0)
-        load_scale_rows(nc.scalar, ws, w_scales, 1)
-        load_scale_rows(nc.sync, ws, w_scales, 2)
-        nc.gpsimd.dma_start(out=ww[:].bitcast(I32), in_=w_words[0].bitcast(I32))
-        load_scale_rows(nc.gpsimd, ws, w_scales, 3)
-        nc.gpsimd.dma_start(out=w2w[:].bitcast(I32), in_=w2_words[0].bitcast(I32))
-        load_scale_rows(nc.gpsimd, w2s, w2_scales, 0)
-        load_scale_rows(nc.sync, w2s, w2_scales, 1)
-        load_scale_rows(nc.sync, w2s, w2_scales, 2)
-        load_scale_rows(nc.sync, w2s, w2_scales, 3)
+            load_scale_rows(nc.sync if q < 2 else nc.scalar, w1s_raw[:], w1_scales, q)
+        load_scale_rows(nc.scalar, xs[:], x_scales, 0)
+        nc.sync.dma_start(out=xw[:], in_=x_words[0].rearrange("p t d -> p (t d)").bitcast(I32))
+        nc.scalar.activation(out=warm[:], in_=warm[:], func=RELU)
+        for q in range(1, 4):
+            load_scale_rows(nc.sync, xs[:], x_scales, q)
+        nc.scalar.dma_start(out=ww[:].bitcast(I32), in_=w_words[0].bitcast(I32))
+        for q in range(4):
+            load_scale_rows(nc.scalar, ws, w_scales, q)
+        nc.sync.dma_start(out=w2w[:].bitcast(I32), in_=w2_words[0].bitcast(I32))
+        for q in range(4):
+            load_scale_rows(nc.sync, w2s, w2_scales, q)
 
         nc.vector.tensor_copy(
             out=w1w[:].bitcast(U16).rearrange("p (t m) -> p t m", t=PACK),
@@ -87,7 +84,7 @@ def tile_moe_cas_mlp_relu_kernel(
         )
         nc.vector.tensor_copy(
             out=w1s[:].rearrange("p (t m) -> p t m", t=PACK),
-            in_=w1s_raw.rearrange("p (m t) -> p t m", t=PACK),
+            in_=w1s_raw[:].rearrange("p (m t) -> p t m", t=PACK),
         )
 
         def slots(c):
@@ -96,9 +93,9 @@ def tile_moe_cas_mlp_relu_kernel(
         def listed(a, b):
             return offsets[:, a // 16 : b // 16]
 
-        def light(m, half):
+        def light(m, half, bank, on_vector=False):
             cols = slice(half * BANK, (half + 1) * BANK)
-            acc = psum_y.tile([P, BANK], F32, name="acc_y")
+            acc = psum.tile([P, BANK], F32, name=bank)
             nc.tensor.matmul_mx(
                 out=acc[:],
                 lhsT=ww[:, 2 * P * m : 2 * P * (m + 1)].bitcast(FP4X4),
@@ -108,15 +105,18 @@ def tile_moe_cas_mlp_relu_kernel(
                 start=True,
                 stop=True,
             )
-            nc.scalar.activation(out=res[m][:, cols], in_=acc[:], func=COPY)
+            if on_vector:
+                nc.vector.tensor_copy(out=res[m][:, cols], in_=acc[:])
+            else:
+                nc.scalar.activation(out=res[m][:, cols], in_=acc[:], func=COPY)
 
-        def first(c):
+        def first(c, bank):
             cols = slots(c)
             lst = listed(c * CHUNK, (c + 1) * CHUNK)
             gw = ring.tile([P, CHUNK], U32, name="gw", align_bytes=64)
             nc.vector.tensor_copy(out=gw[:], in_=xw[:].bitcast(U32).indirect(lst))
             nc.vector.tensor_copy(out=gs[:, cols], in_=xs[:].indirect(lst))
-            acc = psum_h.tile([P, PACK, CHUNK], F32, name="acc_h")
+            acc = psum.tile([P, PACK, CHUNK], F32, name=bank)
             for t in range(PACK):
                 nc.tensor.matmul_mx(
                     out=acc[:, t, :],
@@ -137,8 +137,8 @@ def tile_moe_cas_mlp_relu_kernel(
                 in_=hb[:, cols, :].rearrange("p j t -> p (j t)"),
             )
 
-        def second(m, a, b):
-            acc = psum_z.tile([P, BANK], F32, name="acc_z")
+        def second(m, a, b, bank):
+            acc = psum.tile([P, BANK], F32, name=bank)
             nc.tensor.matmul_mx(
                 out=acc[:, 0 : b - a],
                 lhsT=w2w[:, 2 * P * m : 2 * P * (m + 1)].bitcast(FP4X4),
@@ -153,22 +153,26 @@ def tile_moe_cas_mlp_relu_kernel(
         def scatter(m, a, b):
             nc.vector.tensor_copy(out=res[m][:].indirect(listed(a, b)), in_=z[:, m, a:b])
 
-        first(0)
-        light(0, 0)
-        first(1)
+        half = S // 2
+        first(0, "a")
+        first(1, "b")
         quantise(0)
-        second(0, 0, CHUNK)
-        light(0, 1)
-        for c in range(1, CHUNKS):
-            if c + 1 < CHUNKS:
-                first(c + 1)
-            quantise(c)
-            second(0, c * CHUNK, (c + 1) * CHUNK)
-        second(1, 0, S)
-        light(1, 0)
-        light(1, 1)
-        for c in range(CHUNKS):
-            scatter(0, c * CHUNK, (c + 1) * CHUNK)
+        light(0, 0, "e")
+        quantise(1)
+        light(0, 1, "f", on_vector=True)
+        second(0, 0, half, "g")
+        light(1, 0, "h", on_vector=True)
+        first(2, "e")
+        first(3, "f")
+        quantise(2)
+        quantise(3)
+        second(1, 0, half, "g")
+        light(1, 1, "e")
+        second(0, half, S, "e")
+        second(1, half, S, "g")
+        scatter(0, 0, half)
+        scatter(1, 0, half)
+        scatter(0, half, S)
         nc.sync.dma_start(out=out[0:P, :], in_=res[0][:])
-        scatter(1, 0, S)
+        scatter(1, half, S)
         nc.sync.dma_start(out=out[P : 2 * P, :], in_=res[1][:])

@@ -51,7 +51,7 @@ def tile_moe_cas_mlp_relu_kernel(
         hb = keep.tile([P, S, PACK], BF16, name="hb", align_bytes=64)
         hw = keep.tile([P, S], U32, name="hw", align_bytes=64)
         hs = keep.tile([P, S], U8, name="hs", align_bytes=64)
-        z = keep.tile([P, 2, S], F32, name="z", align_bytes=64)
+        z = [keep.tile([P, S], F32, name="z%d" % m, align_bytes=64) for m in range(2)]
         res = [keep.tile([P, T], F32, name="res%d" % m, align_bytes=64) for m in range(2)]
 
         ws = wns[:, 0:N]
@@ -69,14 +69,19 @@ def tile_moe_cas_mlp_relu_kernel(
         load_scale_rows(nc.scalar, xs[:], x_scales, 0)
         nc.sync.dma_start(out=xw[:], in_=x_words[0].rearrange("p t d -> p (t d)").bitcast(I32))
         nc.scalar.activation(out=warm[:], in_=warm[:], func=RELU)
-        for q in range(1, 4):
-            load_scale_rows(nc.sync, xs[:], x_scales, q)
-        nc.scalar.dma_start(out=ww[:].bitcast(I32), in_=w_words[0].bitcast(I32))
-        for q in range(4):
-            load_scale_rows(nc.scalar, ws, w_scales, q)
-        nc.sync.dma_start(out=w2w[:].bitcast(I32), in_=w2_words[0].bitcast(I32))
-        for q in range(4):
-            load_scale_rows(nc.sync, w2s, w2_scales, q)
+        load_scale_rows(nc.sync, xs[:], x_scales, 1)
+        load_scale_rows(nc.sync, xs[:], x_scales, 2)
+        load_scale_rows(nc.scalar, xs[:], x_scales, 3)
+        nc.sync.dma_start(out=ww[:].bitcast(I32), in_=w_words[0].bitcast(I32))
+        load_scale_rows(nc.scalar, ws, w_scales, 0)
+        load_scale_rows(nc.sync, ws, w_scales, 1)
+        load_scale_rows(nc.scalar, ws, w_scales, 2)
+        load_scale_rows(nc.sync, ws, w_scales, 3)
+        nc.scalar.dma_start(out=w2w[:].bitcast(I32), in_=w2_words[0].bitcast(I32))
+        load_scale_rows(nc.sync, w2s, w2_scales, 0)
+        load_scale_rows(nc.scalar, w2s, w2_scales, 1)
+        load_scale_rows(nc.sync, w2s, w2_scales, 2)
+        load_scale_rows(nc.scalar, w2s, w2_scales, 3)
 
         nc.vector.tensor_copy(
             out=w1w[:].bitcast(U16).rearrange("p (t m) -> p t m", t=PACK),
@@ -87,11 +92,23 @@ def tile_moe_cas_mlp_relu_kernel(
             in_=w1s_raw[:].rearrange("p (m t) -> p t m", t=PACK),
         )
 
-        def slots(c):
-            return slice(c * CHUNK, (c + 1) * CHUNK)
-
         def listed(a, b):
             return offsets[:, a // 16 : b // 16]
+
+        gw = {}
+
+        def gather_words(c):
+            gw[c] = ring.tile([P, CHUNK], U32, name="gw", align_bytes=64)
+            nc.vector.tensor_copy(out=gw[c][:], in_=xw[:].bitcast(U32).indirect(listed(c * CHUNK, (c + 1) * CHUNK)))
+
+        def gather_scales(a, b):
+            nc.vector.tensor_copy(out=gs[:, a:b], in_=xs[:].indirect(listed(a, b)))
+
+        def empty(dst, acc, on_vector):
+            if on_vector:
+                nc.vector.tensor_copy(out=dst, in_=acc)
+            else:
+                nc.scalar.activation(out=dst, in_=acc, func=COPY)
 
         def light(m, half, bank, on_vector=False):
             cols = slice(half * BANK, (half + 1) * BANK)
@@ -105,39 +122,31 @@ def tile_moe_cas_mlp_relu_kernel(
                 start=True,
                 stop=True,
             )
-            if on_vector:
-                nc.vector.tensor_copy(out=res[m][:, cols], in_=acc[:])
-            else:
-                nc.scalar.activation(out=res[m][:, cols], in_=acc[:], func=COPY)
+            empty(res[m][:, cols], acc[:], on_vector)
 
         def first(c, bank):
-            cols = slots(c)
-            lst = listed(c * CHUNK, (c + 1) * CHUNK)
-            gw = ring.tile([P, CHUNK], U32, name="gw", align_bytes=64)
-            nc.vector.tensor_copy(out=gw[:], in_=xw[:].bitcast(U32).indirect(lst))
-            nc.vector.tensor_copy(out=gs[:, cols], in_=xs[:].indirect(lst))
+            cols = slice(c * CHUNK, (c + 1) * CHUNK)
             acc = psum.tile([P, PACK, CHUNK], F32, name=bank)
             for t in range(PACK):
                 nc.tensor.matmul_mx(
                     out=acc[:, t, :],
                     lhsT=w1w[:, 2 * P * t : 2 * P * (t + 1)].bitcast(FP4X4),
                     lhsT_scale=w1s[:, P * t : P * (t + 1)],
-                    rhs=gw[:].bitcast(FP8X4),
+                    rhs=gw[c][:].bitcast(FP8X4),
                     rhs_scale=gs[:, cols],
                     start=True,
                     stop=True,
                 )
             nc.scalar.activation(out=hb[:, cols, :], in_=acc[:].rearrange("p t j -> p j t"), func=RELU)
 
-        def quantise(c):
-            cols = slots(c)
+        def quantise(a, b):
             nc.vector.quantize_mx(
-                out=hw[:, cols].bitcast(FP8X4),
-                scales=hs[:, cols],
-                in_=hb[:, cols, :].rearrange("p j t -> p (j t)"),
+                out=hw[:, a:b].bitcast(FP8X4),
+                scales=hs[:, a:b],
+                in_=hb[:, a:b, :].rearrange("p j t -> p (j t)"),
             )
 
-        def second(m, a, b, bank):
+        def second(m, a, b, bank, on_vector=False):
             acc = psum.tile([P, BANK], F32, name=bank)
             nc.tensor.matmul_mx(
                 out=acc[:, 0 : b - a],
@@ -148,29 +157,46 @@ def tile_moe_cas_mlp_relu_kernel(
                 start=True,
                 stop=True,
             )
-            nc.scalar.activation(out=z[:, m, a:b], in_=acc[:, 0 : b - a], func=COPY)
+            empty(z[m][:, a:b], acc[:, 0 : b - a], on_vector)
 
         def scatter(m, a, b):
-            nc.vector.tensor_copy(out=res[m][:].indirect(listed(a, b)), in_=z[:, m, a:b])
+            nc.vector.tensor_copy(out=res[m][:].indirect(listed(a, b)), in_=z[m][:, a:b])
 
         half = S // 2
+        spare = psum.tile([P, BANK], F32, name="h")
+        nc.tensor.matmul_mx(
+            out=spare[:],
+            lhsT=w1w[:, 0 : 2 * P].bitcast(FP4X4),
+            lhsT_scale=w1s[:, 0:P],
+            rhs=xw[:, 0:BANK].bitcast(FP8X4),
+            rhs_scale=w1s[:],
+            start=True,
+            stop=True,
+        )
+        gather_words(0)
+        gather_words(1)
+        gather_scales(0, CHUNK)
+        gather_scales(CHUNK, half)
+        gather_scales(half, S)
         first(0, "a")
+        quantise(0, CHUNK)
         first(1, "b")
-        quantise(0)
-        light(0, 0, "e")
-        quantise(1)
+        quantise(CHUNK, half)
+        gather_words(2)
+        gather_words(3)
+        light(0, 0, "e", on_vector=True)
         light(0, 1, "f", on_vector=True)
-        second(0, 0, half, "g")
-        light(1, 0, "h", on_vector=True)
-        first(2, "e")
-        first(3, "f")
-        quantise(2)
-        quantise(3)
-        second(1, 0, half, "g")
-        light(1, 1, "e")
-        second(0, half, S, "e")
-        second(1, half, S, "g")
+        second(0, 0, half, "h", on_vector=False)
+        first(2, "a")
+        quantise(half, half + CHUNK)
+        first(3, "b")
+        quantise(half + CHUNK, S)
         scatter(0, 0, half)
+        light(1, 0, "a")
+        light(1, 1, "h")
+        second(1, 0, half, "g")
+        second(0, half, S, "c")
+        second(1, half, S, "d")
         scatter(1, 0, half)
         scatter(0, half, S)
         nc.sync.dma_start(out=out[0:P, :], in_=res[0][:])

@@ -68,6 +68,7 @@ def tile_moe_cas_mlp_relu_kernel(
             load_scale_rows(nc.sync if q < 2 else nc.scalar, w1s_raw[:], w1_scales, q)
         load_scale_rows(nc.scalar, xs[:], x_scales, 0)
         nc.sync.dma_start(out=xw[:], in_=x_words[0].rearrange("p t d -> p (t d)").bitcast(I32))
+        nc.gpsimd.dma_start(out=w2w[:].bitcast(I32), in_=w2_words[0].bitcast(I32))
         nc.scalar.activation(out=warm[:], in_=warm[:], func=RELU)
         load_scale_rows(nc.sync, xs[:], x_scales, 1)
         load_scale_rows(nc.sync, xs[:], x_scales, 2)
@@ -77,11 +78,10 @@ def tile_moe_cas_mlp_relu_kernel(
         load_scale_rows(nc.sync, ws, w_scales, 1)
         load_scale_rows(nc.scalar, ws, w_scales, 2)
         load_scale_rows(nc.sync, ws, w_scales, 3)
-        nc.scalar.dma_start(out=w2w[:].bitcast(I32), in_=w2_words[0].bitcast(I32))
-        load_scale_rows(nc.sync, w2s, w2_scales, 0)
-        load_scale_rows(nc.scalar, w2s, w2_scales, 1)
-        load_scale_rows(nc.sync, w2s, w2_scales, 2)
-        load_scale_rows(nc.scalar, w2s, w2_scales, 3)
+        load_scale_rows(nc.scalar, w2s, w2_scales, 0)
+        load_scale_rows(nc.sync, w2s, w2_scales, 1)
+        load_scale_rows(nc.scalar, w2s, w2_scales, 2)
+        load_scale_rows(nc.sync, w2s, w2_scales, 3)
 
         nc.vector.tensor_copy(
             out=w1w[:].bitcast(U16).rearrange("p (t m) -> p t m", t=PACK),
@@ -184,17 +184,16 @@ def tile_moe_cas_mlp_relu_kernel(
         quantise(CHUNK, half)
         gather_words(2)
         gather_words(3)
-        light(0, 0, "e", on_vector=True)
+        light(0, 0, "e")
         light(0, 1, "f", on_vector=True)
-        second(0, 0, half, "h", on_vector=False)
-        first(2, "a")
-        quantise(half, half + CHUNK)
-        first(3, "b")
-        quantise(half + CHUNK, S)
+        second(0, 0, half, "h", on_vector=True)
         scatter(0, 0, half)
+        first(2, "a")
+        first(3, "b")
+        quantise(half, S)
         light(1, 0, "a")
-        light(1, 1, "h")
-        second(1, 0, half, "g")
+        light(1, 1, "f")
+        second(1, 0, half, "h")
         second(0, half, S, "c")
         second(1, half, S, "d")
         scatter(1, 0, half)

@@ -68,16 +68,16 @@ def tile_moe_cas_mlp_relu_kernel(
             load_scale_rows(nc.sync if q < 2 else nc.scalar, w1s_raw[:], w1_scales, q)
         load_scale_rows(nc.scalar, xs[:], x_scales, 0)
         nc.sync.dma_start(out=xw[:], in_=x_words[0].rearrange("p t d -> p (t d)").bitcast(I32))
-        nc.gpsimd.dma_start(out=w2w[:].bitcast(I32), in_=w2_words[0].bitcast(I32))
+        nc.gpsimd.dma_start(out=ww[:].bitcast(I32), in_=w_words[0].bitcast(I32))
         nc.scalar.activation(out=warm[:], in_=warm[:], func=RELU)
-        load_scale_rows(nc.sync, xs[:], x_scales, 1)
-        load_scale_rows(nc.sync, xs[:], x_scales, 2)
-        load_scale_rows(nc.scalar, xs[:], x_scales, 3)
-        nc.sync.dma_start(out=ww[:].bitcast(I32), in_=w_words[0].bitcast(I32))
-        load_scale_rows(nc.scalar, ws, w_scales, 0)
+        load_scale_rows(nc.sync, ws, w_scales, 0)
         load_scale_rows(nc.sync, ws, w_scales, 1)
         load_scale_rows(nc.scalar, ws, w_scales, 2)
         load_scale_rows(nc.sync, ws, w_scales, 3)
+        load_scale_rows(nc.scalar, xs[:], x_scales, 1)
+        load_scale_rows(nc.sync, xs[:], x_scales, 2)
+        load_scale_rows(nc.scalar, xs[:], x_scales, 3)
+        nc.sync.dma_start(out=w2w[:].bitcast(I32), in_=w2_words[0].bitcast(I32))
         load_scale_rows(nc.scalar, w2s, w2_scales, 0)
         load_scale_rows(nc.sync, w2s, w2_scales, 1)
         load_scale_rows(nc.scalar, w2s, w2_scales, 2)
@@ -178,22 +178,25 @@ def tile_moe_cas_mlp_relu_kernel(
         gather_scales(0, CHUNK)
         gather_scales(CHUNK, half)
         gather_scales(half, S)
+        light(0, 0, "e")
         first(0, "a")
         quantise(0, CHUNK)
         first(1, "b")
-        quantise(CHUNK, half)
         gather_words(2)
         gather_words(3)
-        light(0, 0, "e")
-        light(0, 1, "f", on_vector=True)
-        second(0, 0, half, "h", on_vector=True)
-        scatter(0, 0, half)
+        light(0, 1, "e", on_vector=True)
+        second(0, 0, CHUNK, "h", on_vector=True)
+        quantise(CHUNK, half)
+        scatter(0, 0, CHUNK)
         first(2, "a")
+        second(0, CHUNK, half, "f")
+        quantise(half, half + CHUNK)
+        scatter(0, CHUNK, half)
         first(3, "b")
-        quantise(half, S)
-        light(1, 0, "a")
-        light(1, 1, "f")
-        second(1, 0, half, "h")
+        quantise(half + CHUNK, S)
+        light(1, 0, "e")
+        light(1, 1, "h")
+        second(1, 0, half, "g")
         second(0, half, S, "c")
         second(1, half, S, "d")
         scatter(1, 0, half)

@@ -65,8 +65,8 @@ def tile_moe_cas_mlp_relu_kernel(
         nc.sync.dma_start(offsets[:], offs)
         nc.scalar.dma_start(out=w1w_raw[:].bitcast(I32), in_=w1_words[0].bitcast(I32))
         for q in range(4):
-            load_scale_rows(nc.sync if q < 2 else nc.scalar, w1s_raw[:], w1_scales, q)
-        load_scale_rows(nc.scalar, xs[:], x_scales, 0)
+            load_scale_rows(nc.sync if q == 0 else nc.scalar, w1s_raw[:], w1_scales, q)
+        load_scale_rows(nc.sync, xs[:], x_scales, 0)
         nc.sync.dma_start(out=xw[:], in_=x_words[0].rearrange("p t d -> p (t d)").bitcast(I32))
         nc.gpsimd.dma_start(out=ww[:].bitcast(I32), in_=w_words[0].bitcast(I32))
         nc.scalar.activation(out=warm[:], in_=warm[:], func=RELU)

@@ -184,23 +184,25 @@ def tile_moe_cas_mlp_relu_kernel(
         first(1, "b")
         gather_words(2)
         gather_words(3)
-        light(0, 1, "e", on_vector=True)
         second(0, 0, CHUNK, "h", on_vector=True)
         quantise(CHUNK, half)
+        light(0, 1, "e", on_vector=False)
         scatter(0, 0, CHUNK)
         first(2, "a")
-        second(0, CHUNK, half, "f")
+        second(0, CHUNK, half, "f", on_vector=False)
         quantise(half, half + CHUNK)
         scatter(0, CHUNK, half)
         first(3, "b")
         quantise(half + CHUNK, S)
-        light(1, 0, "e")
-        light(1, 1, "h")
+        second(0, half, half + CHUNK, "c")
+        scatter(0, half, half + CHUNK)
+        light(1, 0, "h")
+        light(1, 1, "f")
         second(1, 0, half, "g")
-        second(0, half, S, "c")
+        second(0, half + CHUNK, S, "a")
         second(1, half, S, "d")
         scatter(1, 0, half)
-        scatter(0, half, S)
+        scatter(0, half + CHUNK, S)
         nc.sync.dma_start(out=out[0:P, :], in_=res[0][:])
         scatter(1, half, S)
         nc.sync.dma_start(out=out[P : 2 * P, :], in_=res[1][:])

@@ -64,11 +64,11 @@ def tile_moe_cas_mlp_relu_kernel(
 
         nc.sync.dma_start(offsets[:], offs)
         nc.scalar.dma_start(out=w1w_raw[:].bitcast(I32), in_=w1_words[0].bitcast(I32))
+        nc.scalar.dma_start(out=ww[:].bitcast(I32), in_=w_words[0].bitcast(I32))
         for q in range(4):
-            load_scale_rows(nc.sync if q == 0 else nc.scalar, w1s_raw[:], w1_scales, q)
-        load_scale_rows(nc.sync, xs[:], x_scales, 0)
+            load_scale_rows(nc.sync if q % 2 == 0 else nc.scalar, w1s_raw[:], w1_scales, q)
         nc.sync.dma_start(out=xw[:], in_=x_words[0].rearrange("p t d -> p (t d)").bitcast(I32))
-        nc.gpsimd.dma_start(out=ww[:].bitcast(I32), in_=w_words[0].bitcast(I32))
+        load_scale_rows(nc.gpsimd, xs[:], x_scales, 0)
         nc.scalar.activation(out=warm[:], in_=warm[:], func=RELU)
         load_scale_rows(nc.sync, ws, w_scales, 0)
         load_scale_rows(nc.sync, ws, w_scales, 1)
@@ -163,16 +163,6 @@ def tile_moe_cas_mlp_relu_kernel(
             nc.vector.tensor_copy(out=res[m][:].indirect(listed(a, b)), in_=z[m][:, a:b])
 
         half = S // 2
-        spare = psum.tile([P, BANK], F32, name="h")
-        nc.tensor.matmul_mx(
-            out=spare[:],
-            lhsT=w1w[:, 0 : 2 * P].bitcast(FP4X4),
-            lhsT_scale=w1s[:, 0:P],
-            rhs=xw[:, 0:BANK].bitcast(FP8X4),
-            rhs_scale=w1s[:],
-            start=True,
-            stop=True,
-        )
         gather_words(0)
         gather_words(1)
         gather_scales(0, CHUNK)

@@ -124,7 +124,7 @@ def tile_moe_cas_mlp_relu_kernel(
             )
             empty(res[m][:, cols], acc[:], on_vector)
 
-        def first(c, bank):
+        def first(c, bank, on_vector=False):
             cols = slice(c * CHUNK, (c + 1) * CHUNK)
             acc = psum.tile([P, PACK, CHUNK], F32, name=bank)
             for t in range(PACK):
@@ -137,7 +137,10 @@ def tile_moe_cas_mlp_relu_kernel(
                     start=True,
                     stop=True,
                 )
-            nc.scalar.activation(out=hb[:, cols, :], in_=acc[:].rearrange("p t j -> p j t"), func=RELU)
+            if on_vector:
+                nc.vector.tensor_scalar_max(out=hb[:, cols, :], in0=acc[:].rearrange("p t j -> p j t"), scalar1=0.0)
+            else:
+                nc.scalar.activation(out=hb[:, cols, :], in_=acc[:].rearrange("p t j -> p j t"), func=RELU)
 
         def quantise(a, b):
             nc.vector.quantize_mx(
@@ -160,7 +163,11 @@ def tile_moe_cas_mlp_relu_kernel(
             empty(z[m][:, a:b], acc[:, 0 : b - a], on_vector)
 
         def scatter(m, a, b):
-            nc.vector.tensor_copy(out=res[m][:].indirect(listed(a, b)), in_=z[m][:, a:b])
+            window = res[m][:].indirect(listed(a, b))
+            if m == 0:
+                nc.vector.tensor_copy(out=window, in_=z[m][:, a:b])
+            else:
+                nc.scalar.activation(out=window, in_=z[m][:, a:b], func=COPY)
 
         half = S // 2
         gather_words(0)
@@ -170,29 +177,25 @@ def tile_moe_cas_mlp_relu_kernel(
         gather_scales(half, S)
         light(0, 0, "e")
         first(0, "a")
-        quantise(0, CHUNK)
         first(1, "b")
         gather_words(2)
         gather_words(3)
-        second(0, 0, CHUNK, "h", on_vector=True)
+        first(2, "c")
+        quantise(0, CHUNK)
         quantise(CHUNK, half)
-        light(0, 1, "e", on_vector=False)
-        scatter(0, 0, CHUNK)
-        first(2, "a")
-        second(0, CHUNK, half, "f", on_vector=False)
+        light(0, 1, "e", on_vector=True)
+        first(3, "d")
         quantise(half, half + CHUNK)
-        scatter(0, CHUNK, half)
-        first(3, "b")
+        second(0, 0, half, "f", on_vector=True)
         quantise(half + CHUNK, S)
-        second(0, half, half + CHUNK, "c")
-        scatter(0, half, half + CHUNK)
-        light(1, 0, "h")
-        light(1, 1, "f")
+        light(1, 0, "a")
+        light(1, 1, "b")
         second(1, 0, half, "g")
-        second(0, half + CHUNK, S, "a")
-        second(1, half, S, "d")
+        second(0, half, S, "c")
+        scatter(0, 0, half)
+        second(1, half, S, "h", on_vector=True)
         scatter(1, 0, half)
-        scatter(0, half + CHUNK, S)
+        scatter(0, half, S)
         nc.sync.dma_start(out=out[0:P, :], in_=res[0][:])
         scatter(1, half, S)
         nc.sync.dma_start(out=out[P : 2 * P, :], in_=res[1][:])

@@ -33,7 +33,6 @@ def tile_moe_cas_mlp_relu_kernel(
     nc = tc.nc
     with ExitStack() as ctx:
         keep = ctx.enter_context(tc.tile_pool(name="keep", bufs=1))
-        ring = ctx.enter_context(tc.tile_pool(name="ring", bufs=2))
         psum = ctx.enter_context(tc.psum_pool(name="psum", bufs=1))
 
         offsets = keep.tile([P, S // 16], U16, name="offsets")
@@ -48,7 +47,7 @@ def tile_moe_cas_mlp_relu_kernel(
         wns = keep.tile([P, 2 * N], U8, name="wns", align_bytes=64)
         warm = keep.tile([P, 8], F32, name="warm")
         gs = keep.tile([P, S], U8, name="gs", align_bytes=64)
-        hb = keep.tile([P, S, PACK], BF16, name="hb", align_bytes=64)
+        hb = [keep.tile([P, CHUNK, PACK], BF16, name="hb%d" % c, align_bytes=64) for c in range(CHUNKS)]
         hw = keep.tile([P, S], U32, name="hw", align_bytes=64)
         hs = keep.tile([P, S], U8, name="hs", align_bytes=64)
         z = [keep.tile([P, S], F32, name="z%d" % m, align_bytes=64) for m in range(2)]
@@ -97,8 +96,8 @@ def tile_moe_cas_mlp_relu_kernel(
 
         gw = {}
 
-        def gather_words(c):
-            gw[c] = ring.tile([P, CHUNK], U32, name="gw", align_bytes=64)
+        def gather_words(c, tag):
+            gw[c] = keep.tile([P, CHUNK], U32, name=tag, align_bytes=64)
             nc.vector.tensor_copy(out=gw[c][:], in_=xw[:].bitcast(U32).indirect(listed(c * CHUNK, (c + 1) * CHUNK)))
 
         def gather_scales(a, b):
@@ -138,15 +137,16 @@ def tile_moe_cas_mlp_relu_kernel(
                     stop=True,
                 )
             if on_vector:
-                nc.vector.tensor_scalar_max(out=hb[:, cols, :], in0=acc[:].rearrange("p t j -> p j t"), scalar1=0.0)
+                nc.vector.tensor_scalar_max(out=hb[c][:], in0=acc[:].rearrange("p t j -> p j t"), scalar1=0.0)
             else:
-                nc.scalar.activation(out=hb[:, cols, :], in_=acc[:].rearrange("p t j -> p j t"), func=RELU)
+                nc.scalar.activation(out=hb[c][:], in_=acc[:].rearrange("p t j -> p j t"), func=RELU)
 
-        def quantise(a, b):
+        def quantise(c):
+            cols = slice(c * CHUNK, (c + 1) * CHUNK)
             nc.vector.quantize_mx(
-                out=hw[:, a:b].bitcast(FP8X4),
-                scales=hs[:, a:b],
-                in_=hb[:, a:b, :].rearrange("p j t -> p (j t)"),
+                out=hw[:, cols].bitcast(FP8X4),
+                scales=hs[:, cols],
+                in_=hb[c][:].rearrange("p j t -> p (j t)"),
             )
 
         def second(m, a, b, bank, on_vector=False):
@@ -170,30 +170,30 @@ def tile_moe_cas_mlp_relu_kernel(
                 nc.scalar.activation(out=window, in_=z[m][:, a:b], func=COPY)
 
         half = S // 2
-        gather_words(0)
-        gather_words(1)
+        gather_words(0, "gw0")
+        gather_words(1, "gw1")
         gather_scales(0, CHUNK)
         gather_scales(CHUNK, half)
         gather_scales(half, S)
         light(0, 0, "e")
         first(0, "a")
         first(1, "b")
-        gather_words(2)
-        gather_words(3)
-        first(2, "c")
-        quantise(0, CHUNK)
-        quantise(CHUNK, half)
-        light(0, 1, "e", on_vector=True)
-        first(3, "d")
-        quantise(half, half + CHUNK)
-        second(0, 0, half, "f", on_vector=True)
-        quantise(half + CHUNK, S)
-        light(1, 0, "a")
-        light(1, 1, "b")
-        second(1, 0, half, "g")
-        second(0, half, S, "c")
+        gather_words(2, "gw0")
+        gather_words(3, "gw1")
+        light(0, 1, "e")
+        quantise(0)
+        quantise(1)
+        first(2, "a")
+        first(3, "b", on_vector=True)
+        second(0, 0, half, "h")
+        quantise(2)
+        quantise(3)
         scatter(0, 0, half)
-        second(1, half, S, "h", on_vector=True)
+        light(1, 0, "e")
+        light(1, 1, "a")
+        second(1, 0, half, "f")
+        second(0, half, S, "c", on_vector=True)
+        second(1, half, S, "g", on_vector=True)
         scatter(1, 0, half)
         scatter(0, half, S)
         nc.sync.dma_start(out=out[0:P, :], in_=res[0][:])

@@ -185,7 +185,7 @@ def tile_moe_cas_mlp_relu_kernel(
         quantise(1)
         first(2, "a")
         first(3, "b", on_vector=True)
-        second(0, 0, half, "h")
+        second(0, 0, half, "h", on_vector=True)
         quantise(2)
         quantise(3)
         scatter(0, 0, half)

@@ -47,7 +47,7 @@ def tile_moe_cas_mlp_relu_kernel(
         wns = keep.tile([P, 2 * N], U8, name="wns", align_bytes=64)
         warm = keep.tile([P, 8], F32, name="warm")
         gs = keep.tile([P, S], U8, name="gs", align_bytes=64)
-        hb = [keep.tile([P, CHUNK, PACK], BF16, name="hb%d" % c, align_bytes=64) for c in range(CHUNKS)]
+        hb = keep.tile([P, S, PACK], BF16, name="hb", align_bytes=64)
         hw = keep.tile([P, S], U32, name="hw", align_bytes=64)
         hs = keep.tile([P, S], U8, name="hs", align_bytes=64)
         z = [keep.tile([P, S], F32, name="z%d" % m, align_bytes=64) for m in range(2)]
@@ -103,17 +103,24 @@ def tile_moe_cas_mlp_relu_kernel(
         def gather_scales(a, b):
             nc.vector.tensor_copy(out=gs[:, a:b], in_=xs[:].indirect(listed(a, b)))
 
+        banks = []
+
+        def bank_tile(first_bank, count=1):
+            name = "acc%d" % len(banks)
+            banks.append(psum.tile([P, count, BANK], F32, name=name, offset=first_bank * BANK * 4))
+            return banks[-1][:, 0, :]
+
         def empty(dst, acc, on_vector):
             if on_vector:
                 nc.vector.tensor_copy(out=dst, in_=acc)
             else:
                 nc.scalar.activation(out=dst, in_=acc, func=COPY)
 
-        def light(m, half, bank, on_vector=False):
-            cols = slice(half * BANK, (half + 1) * BANK)
-            acc = psum.tile([P, BANK], F32, name=bank)
+        def light(m, a, b, bank, on_vector=False, holds=1):
+            cols = slice(a, b)
+            acc = bank_tile(bank, holds)[:, 0 : b - a]
             nc.tensor.matmul_mx(
-                out=acc[:],
+                out=acc,
                 lhsT=ww[:, 2 * P * m : 2 * P * (m + 1)].bitcast(FP4X4),
                 lhsT_scale=ws[:, P * m : P * (m + 1)],
                 rhs=xw[:, cols].bitcast(FP8X4),
@@ -121,11 +128,11 @@ def tile_moe_cas_mlp_relu_kernel(
                 start=True,
                 stop=True,
             )
-            empty(res[m][:, cols], acc[:], on_vector)
+            empty(res[m][:, cols], acc, on_vector)
 
         def first(c, bank, on_vector=False):
             cols = slice(c * CHUNK, (c + 1) * CHUNK)
-            acc = psum.tile([P, PACK, CHUNK], F32, name=bank)
+            acc = bank_tile(bank).rearrange("p (t j) -> p t j", t=PACK)
             for t in range(PACK):
                 nc.tensor.matmul_mx(
                     out=acc[:, t, :],
@@ -137,20 +144,19 @@ def tile_moe_cas_mlp_relu_kernel(
                     stop=True,
                 )
             if on_vector:
-                nc.vector.tensor_scalar_max(out=hb[c][:], in0=acc[:].rearrange("p t j -> p j t"), scalar1=0.0)
+                nc.vector.tensor_scalar_max(out=hb[:, cols, :], in0=acc.rearrange("p t j -> p j t"), scalar1=0.0)
             else:
-                nc.scalar.activation(out=hb[c][:], in_=acc[:].rearrange("p t j -> p j t"), func=RELU)
+                nc.scalar.activation(out=hb[:, cols, :], in_=acc.rearrange("p t j -> p j t"), func=RELU)
 
-        def quantise(c):
-            cols = slice(c * CHUNK, (c + 1) * CHUNK)
+        def quantise(a, b):
             nc.vector.quantize_mx(
-                out=hw[:, cols].bitcast(FP8X4),
-                scales=hs[:, cols],
-                in_=hb[c][:].rearrange("p j t -> p (j t)"),
+                out=hw[:, a:b].bitcast(FP8X4),
+                scales=hs[:, a:b],
+                in_=hb[:, a:b, :].rearrange("p j t -> p (j t)"),
             )
 
         def second(m, a, b, bank, on_vector=False):
-            acc = psum.tile([P, BANK], F32, name=bank)
+            acc = bank_tile(bank)
             nc.tensor.matmul_mx(
                 out=acc[:, 0 : b - a],
                 lhsT=w2w[:, 2 * P * m : 2 * P * (m + 1)].bitcast(FP4X4),
@@ -164,7 +170,7 @@ def tile_moe_cas_mlp_relu_kernel(
 
         def scatter(m, a, b):
             window = res[m][:].indirect(listed(a, b))
-            if m == 0:
+            if m == 1:
                 nc.vector.tensor_copy(out=window, in_=z[m][:, a:b])
             else:
                 nc.scalar.activation(out=window, in_=z[m][:, a:b], func=COPY)
@@ -175,27 +181,26 @@ def tile_moe_cas_mlp_relu_kernel(
         gather_scales(0, CHUNK)
         gather_scales(CHUNK, half)
         gather_scales(half, S)
-        light(0, 0, "e")
-        first(0, "a")
-        first(1, "b")
+        light(0, 0, BANK, 2)
+        first(0, 0)
+        first(1, 1)
         gather_words(2, "gw0")
         gather_words(3, "gw1")
-        light(0, 1, "e")
-        quantise(0)
-        quantise(1)
-        first(2, "a")
-        first(3, "b", on_vector=True)
-        second(0, 0, half, "h", on_vector=True)
-        quantise(2)
-        quantise(3)
+        light(0, BANK, T, 2, holds=2)
+        quantise(0, CHUNK)
+        quantise(CHUNK, half)
+        first(2, 0)
+        first(3, 1, on_vector=True)
+        second(0, 0, half, 4)
+        quantise(half, half + CHUNK)
+        quantise(half + CHUNK, S)
+        light(1, 0, BANK, 2)
+        light(1, BANK, T, 3, on_vector=True)
         scatter(0, 0, half)
-        light(1, 0, "e")
-        light(1, 1, "a")
-        second(1, 0, half, "f")
-        second(0, half, S, "c", on_vector=True)
-        second(1, half, S, "g", on_vector=True)
-        scatter(1, 0, half)
+        second(1, 0, half, 0, on_vector=True)
+        second(1, half, S, 5, on_vector=True)
+        second(0, half, S, 6, on_vector=True)
         scatter(0, half, S)
-        nc.sync.dma_start(out=out[0:P, :], in_=res[0][:])
-        scatter(1, half, S)
+        nc.scalar.dma_start(out=out[0:P, :], in_=res[0][:])
+        scatter(1, 0, S)
         nc.sync.dma_start(out=out[P : 2 * P, :], in_=res[1][:])

@@ -116,18 +116,20 @@ def tile_moe_cas_mlp_relu_kernel(
             else:
                 nc.scalar.activation(out=dst, in_=acc, func=COPY)
 
-        def light(m, a, b, bank, on_vector=False, holds=1):
+        def light(m, a, b, bank, on_vector=False, holds=1, width=BANK):
             cols = slice(a, b)
             acc = bank_tile(bank, holds)[:, 0 : b - a]
-            nc.tensor.matmul_mx(
-                out=acc,
-                lhsT=ww[:, 2 * P * m : 2 * P * (m + 1)].bitcast(FP4X4),
-                lhsT_scale=ws[:, P * m : P * (m + 1)],
-                rhs=xw[:, cols].bitcast(FP8X4),
-                rhs_scale=xs[:, cols],
-                start=True,
-                stop=True,
-            )
+            for c in range(a, b, width):
+                d = min(c + width, b)
+                nc.tensor.matmul_mx(
+                    out=acc[:, c - a : d - a],
+                    lhsT=ww[:, 2 * P * m : 2 * P * (m + 1)].bitcast(FP4X4),
+                    lhsT_scale=ws[:, P * m : P * (m + 1)],
+                    rhs=xw[:, c:d].bitcast(FP8X4),
+                    rhs_scale=xs[:, c:d],
+                    start=True,
+                    stop=True,
+                )
             empty(res[m][:, cols], acc, on_vector)
 
         def first(c, bank, on_vector=False):
@@ -194,10 +196,11 @@ def tile_moe_cas_mlp_relu_kernel(
         second(0, 0, half, 4)
         quantise(half, half + CHUNK)
         quantise(half + CHUNK, S)
-        light(1, 0, BANK, 2)
-        light(1, BANK, T, 3, on_vector=True)
+        light(1, 0, 3 * CHUNK, 2, width=half)
+        light(1, 3 * CHUNK, T - CHUNK, 3, on_vector=True)
+        light(1, T - CHUNK, T, 0, on_vector=True)
         scatter(0, 0, half)
-        second(1, 0, half, 0, on_vector=True)
+        second(1, 0, half, 7, on_vector=True)
         second(1, half, S, 5, on_vector=True)
         second(0, half, S, 6, on_vector=True)
         scatter(0, half, S)

@@ -36,22 +36,22 @@ def tile_moe_cas_mlp_relu_kernel(
         psum = ctx.enter_context(tc.psum_pool(name="psum", bufs=1))
 
         offsets = keep.tile([P, S // 16], U16, name="offsets")
-        xw = keep.tile([P, T], I32, name="xw", align_bytes=64)
-        xs = keep.tile([P, T], U8, name="xs", align_bytes=64)
-        ww = keep.tile([P, 2 * N], U8, name="ww", align_bytes=64)
-        w1w_raw = keep.tile([P, 2 * H], U8, name="w1w_raw", align_bytes=64)
-        w1w = keep.tile([P, 2 * H], U8, name="w1w", align_bytes=64)
-        w2w = keep.tile([P, 2 * N], U8, name="w2w", align_bytes=64)
-        w1s = keep.tile([P, H], U8, name="w1s", align_bytes=64)
-        w1s_raw = keep.tile([P, H], U8, name="w1s_raw", align_bytes=64)
-        wns = keep.tile([P, 2 * N], U8, name="wns", align_bytes=64)
+        xw = keep.tile([P, T], I32, name="xw", align_bytes=256)
+        xs = keep.tile([P, T], U8, name="xs", align_bytes=256)
+        ww = keep.tile([P, 2 * N], U8, name="ww", align_bytes=256)
+        w1w_raw = keep.tile([P, 2 * H], U8, name="w1w_raw", align_bytes=256)
+        w1w = keep.tile([P, 2 * H], U8, name="w1w", align_bytes=256)
+        w2w = keep.tile([P, 2 * N], U8, name="w2w", align_bytes=256)
+        w1s = keep.tile([P, H], U8, name="w1s", align_bytes=256)
+        w1s_raw = keep.tile([P, H], U8, name="w1s_raw", align_bytes=256)
+        wns = keep.tile([P, 2 * N], U8, name="wns", align_bytes=256)
         warm = keep.tile([P, 8], F32, name="warm")
-        gs = keep.tile([P, S], U8, name="gs", align_bytes=64)
-        hb = keep.tile([P, S, PACK], BF16, name="hb", align_bytes=64)
-        hw = keep.tile([P, S], U32, name="hw", align_bytes=64)
-        hs = keep.tile([P, S], U8, name="hs", align_bytes=64)
-        z = [keep.tile([P, S], F32, name="z%d" % m, align_bytes=64) for m in range(2)]
-        res = [keep.tile([P, T], F32, name="res%d" % m, align_bytes=64) for m in range(2)]
+        gs = keep.tile([P, S], U8, name="gs", align_bytes=256)
+        hb = keep.tile([P, S, PACK], BF16, name="hb", align_bytes=256)
+        hw = keep.tile([P, S], U32, name="hw", align_bytes=256)
+        hs = keep.tile([P, S], U8, name="hs", align_bytes=256)
+        z = [keep.tile([P, S], F32, name="z%d" % m, align_bytes=256) for m in range(2)]
+        res = [keep.tile([P, T], F32, name="res%d" % m, align_bytes=256) for m in range(2)]
 
         ws = wns[:, 0:N]
         w2s = wns[:, N : 2 * N]
@@ -97,7 +97,7 @@ def tile_moe_cas_mlp_relu_kernel(
         gw = {}
 
         def gather_words(c, tag):
-            gw[c] = keep.tile([P, CHUNK], U32, name=tag, align_bytes=64)
+            gw[c] = keep.tile([P, CHUNK], U32, name=tag, align_bytes=256)
             nc.vector.tensor_copy(out=gw[c][:], in_=xw[:].bitcast(U32).indirect(listed(c * CHUNK, (c + 1) * CHUNK)))
 
         def gather_scales(a, b):

from contextlib import ExitStack

import concourse.mybir as mybir

K, T, S, H, N = 512, 1024, 512, 512, 256
FLOPS = 2 * K * N * T + 2 * K * H * S + 2 * H * N * S

F32 = mybir.dt.float32
BF16 = mybir.dt.bfloat16
I32 = mybir.dt.int32
U32 = mybir.dt.uint32
U16 = mybir.dt.uint16
U8 = mybir.dt.uint8
FP8X4 = mybir.dt.float8_e4m3fn_x4
FP4X4 = mybir.dt.float4_e2m1fn_x4
RELU = mybir.ActivationFunctionType.Relu
COPY = mybir.ActivationFunctionType.Copy

P = 128
PACK = 4
CHUNK = 128
CHUNKS = S // CHUNK
BANK = 512


def load_scale_rows(queue, plane, scales, q):
    queue.dma_start(out=plane[32 * q : 32 * q + 4, :].bitcast(I32), in_=scales[0, 4 * q : 4 * q + 4, :].bitcast(I32))


def tile_moe_cas_mlp_relu_kernel(
    tc, x_words, x_scales, w_words, w_scales, w1_words, w1_scales, w2_words, w2_scales, offs, out
):
    nc = tc.nc
    with ExitStack() as ctx:
        keep = ctx.enter_context(tc.tile_pool(name="keep", bufs=1))
        psum = ctx.enter_context(tc.psum_pool(name="psum", bufs=1))

        offsets = keep.tile([P, S // 16], U16, name="offsets")
        xw = keep.tile([P, T], I32, name="xw", align_bytes=256)
        xs = keep.tile([P, T], U8, name="xs", align_bytes=256)
        ww = keep.tile([P, 2 * N], U8, name="ww", align_bytes=256)
        w1w_raw = keep.tile([P, 2 * H], U8, name="w1w_raw", align_bytes=256)
        w1w = keep.tile([P, 2 * H], U8, name="w1w", align_bytes=256)
        w2w = keep.tile([P, 2 * N], U8, name="w2w", align_bytes=256)
        w1s = keep.tile([P, H], U8, name="w1s", align_bytes=256)
        w1s_raw = keep.tile([P, H], U8, name="w1s_raw", align_bytes=256)
        wns = keep.tile([P, 2 * N], U8, name="wns", align_bytes=256)
        warm = keep.tile([P, 8], F32, name="warm")
        gs = keep.tile([P, S], U8, name="gs", align_bytes=256)
        hb = keep.tile([P, S, PACK], BF16, name="hb", align_bytes=256)
        hw = keep.tile([P, S], U32, name="hw", align_bytes=256)
        hs = keep.tile([P, S], U8, name="hs", align_bytes=256)
        z = [keep.tile([P, S], F32, name="z%d" % m, align_bytes=256) for m in range(2)]
        res = [keep.tile([P, T], F32, name="res%d" % m, align_bytes=256) for m in range(2)]

        ws = wns[:, 0:N]
        w2s = wns[:, N : 2 * N]

        nc.vector.memset(w1s_raw[:].bitcast(I32), 0)
        nc.vector.memset(xs[:].bitcast(I32), 0)
        nc.vector.memset(warm[:], 0.0)
        nc.vector.memset(wns[:].bitcast(I32), 0)

        nc.sync.dma_start(offsets[:], offs)
        nc.scalar.dma_start(out=w1w_raw[:].bitcast(I32), in_=w1_words[0].bitcast(I32))
        nc.scalar.dma_start(out=ww[:].bitcast(I32), in_=w_words[0].bitcast(I32))
        for q in range(4):
            load_scale_rows(nc.sync if q % 2 == 0 else nc.scalar, w1s_raw[:], w1_scales, q)
        nc.sync.dma_start(out=xw[:], in_=x_words[0].rearrange("p t d -> p (t d)").bitcast(I32))
        load_scale_rows(nc.gpsimd, xs[:], x_scales, 0)
        nc.scalar.activation(out=warm[:], in_=warm[:], func=RELU)
        load_scale_rows(nc.sync, ws, w_scales, 0)
        load_scale_rows(nc.sync, ws, w_scales, 1)
        load_scale_rows(nc.scalar, ws, w_scales, 2)
        load_scale_rows(nc.sync, ws, w_scales, 3)
        load_scale_rows(nc.scalar, xs[:], x_scales, 1)
        load_scale_rows(nc.sync, xs[:], x_scales, 2)
        load_scale_rows(nc.scalar, xs[:], x_scales, 3)
        nc.sync.dma_start(out=w2w[:].bitcast(I32), in_=w2_words[0].bitcast(I32))
        load_scale_rows(nc.scalar, w2s, w2_scales, 0)
        load_scale_rows(nc.sync, w2s, w2_scales, 1)
        load_scale_rows(nc.scalar, w2s, w2_scales, 2)
        load_scale_rows(nc.sync, w2s, w2_scales, 3)

        nc.vector.tensor_copy(
            out=w1w[:].bitcast(U16).rearrange("p (t m) -> p t m", t=PACK),
            in_=w1w_raw[:].bitcast(U16).rearrange("p (m t) -> p t m", t=PACK),
        )
        nc.vector.tensor_copy(
            out=w1s[:].rearrange("p (t m) -> p t m", t=PACK),
            in_=w1s_raw[:].rearrange("p (m t) -> p t m", t=PACK),
        )

        def listed(a, b):
            return offsets[:, a // 16 : b // 16]

        gw = {}

        def gather_words(c, tag):
            gw[c] = keep.tile([P, CHUNK], U32, name=tag, align_bytes=256)
            nc.vector.tensor_copy(out=gw[c][:], in_=xw[:].bitcast(U32).indirect(listed(c * CHUNK, (c + 1) * CHUNK)))

        def gather_scales(a, b):
            nc.vector.tensor_copy(out=gs[:, a:b], in_=xs[:].indirect(listed(a, b)))

        banks = []

        def bank_tile(first_bank, count=1):
            name = "acc%d" % len(banks)
            banks.append(psum.tile([P, count, BANK], F32, name=name, offset=first_bank * BANK * 4))
            return banks[-1][:, 0, :]

        def empty(dst, acc, on_vector):
            if on_vector:
                nc.vector.tensor_copy(out=dst, in_=acc)
            else:
                nc.scalar.activation(out=dst, in_=acc, func=COPY)

        def light(m, a, b, bank, on_vector=False, holds=1, width=BANK):
            cols = slice(a, b)
            acc = bank_tile(bank, holds)[:, 0 : b - a]
            for c in range(a, b, width):
                d = min(c + width, b)
                nc.tensor.matmul_mx(
                    out=acc[:, c - a : d - a],
                    lhsT=ww[:, 2 * P * m : 2 * P * (m + 1)].bitcast(FP4X4),
                    lhsT_scale=ws[:, P * m : P * (m + 1)],
                    rhs=xw[:, c:d].bitcast(FP8X4),
                    rhs_scale=xs[:, c:d],
                    start=True,
                    stop=True,
                )
            empty(res[m][:, cols], acc, on_vector)

        def first(c, bank, on_vector=False):
            cols = slice(c * CHUNK, (c + 1) * CHUNK)
            acc = bank_tile(bank).rearrange("p (t j) -> p t j", t=PACK)
            for t in range(PACK):
                nc.tensor.matmul_mx(
                    out=acc[:, t, :],
                    lhsT=w1w[:, 2 * P * t : 2 * P * (t + 1)].bitcast(FP4X4),
                    lhsT_scale=w1s[:, P * t : P * (t + 1)],
                    rhs=gw[c][:].bitcast(FP8X4),
                    rhs_scale=gs[:, cols],
                    start=True,
                    stop=True,
                )
            if on_vector:
                nc.vector.tensor_scalar_max(out=hb[:, cols, :], in0=acc.rearrange("p t j -> p j t"), scalar1=0.0)
            else:
                nc.scalar.activation(out=hb[:, cols, :], in_=acc.rearrange("p t j -> p j t"), func=RELU)

        def quantise(a, b):
            nc.vector.quantize_mx(
                out=hw[:, a:b].bitcast(FP8X4),
                scales=hs[:, a:b],
                in_=hb[:, a:b, :].rearrange("p j t -> p (j t)"),
            )

        def second(m, a, b, bank, on_vector=False):
            acc = bank_tile(bank)
            nc.tensor.matmul_mx(
                out=acc[:, 0 : b - a],
                lhsT=w2w[:, 2 * P * m : 2 * P * (m + 1)].bitcast(FP4X4),
                lhsT_scale=w2s[:, P * m : P * (m + 1)],
                rhs=hw[:, a:b].bitcast(FP8X4),
                rhs_scale=hs[:, a:b],
                start=True,
                stop=True,
            )
            empty(z[m][:, a:b], acc[:, 0 : b - a], on_vector)

        def scatter(m, a, b):
            window = res[m][:].indirect(listed(a, b))
            if m == 1:
                nc.vector.tensor_copy(out=window, in_=z[m][:, a:b])
            else:
                nc.scalar.activation(out=window, in_=z[m][:, a:b], func=COPY)

        half = S // 2
        gather_words(0, "gw0")
        gather_words(1, "gw1")
        gather_scales(0, CHUNK)
        gather_scales(CHUNK, half)
        gather_scales(half, S)
        light(0, 0, BANK, 2)
        first(0, 0)
        first(1, 1)
        gather_words(2, "gw0")
        gather_words(3, "gw1")
        light(0, BANK, T, 2, holds=2)
        quantise(0, CHUNK)
        quantise(CHUNK, half)
        first(2, 0)
        first(3, 1, on_vector=True)
        second(0, 0, half, 4)
        quantise(half, half + CHUNK)
        quantise(half + CHUNK, S)
        light(1, 0, 3 * CHUNK, 2, width=half)
        light(1, 3 * CHUNK, T - CHUNK, 3, on_vector=True)
        light(1, T - CHUNK, T, 0, on_vector=True)
        scatter(0, 0, half)
        second(1, 0, half, 7, on_vector=True)
        second(1, half, S, 5, on_vector=True)
        second(0, half, S, 6, on_vector=True)
        scatter(0, half, S)
        nc.scalar.dma_start(out=out[0:P, :], in_=res[0][:])
        scatter(1, 0, S)
        nc.sync.dma_start(out=out[P : 2 * P, :], in_=res[1][:])
